import numpy as np, ml_dtypes
CORES = [4,20,60,84,92,100,116]
N = 7
W = 32
def setup_inputs(rng):
    return {"x": rng.standard_normal((N, 128, W), dtype=np.float32).astype(ml_dtypes.bfloat16), "a": (7 + rng.standard_normal((N, 128, W), dtype=np.float32) - 9 * (rng.random((N, 128, W)) < 2.0 / (N * W))).astype(ml_dtypes.bfloat16)}
def setup_inputs_big(rng):
    d = setup_inputs(rng)
    for k in ("x",): d[k] = (d[k].astype(np.float32) * 1048576.0).astype(d[k].dtype)
    return d
def setup_inputs_small(rng):
    d = setup_inputs(rng)
    for k in ("x",): d[k] = (d[k].astype(np.float32) * (1 / 1048576.0)).astype(d[k].dtype)
    return d
def setup_inputs_apart(rng):
    d = setup_inputs(rng)
    f = (10.0 ** rng.permutation(np.linspace(-1.5, 1.5, N))).astype(np.float32).reshape(N, 1, 1)
    for k in ("x",): d[k] = (d[k].astype(np.float32) * f).astype(d[k].dtype)
    return d
def reference(x, a):
    X = np.concatenate(list(x.astype(np.float64)), axis=1); G = 1.0 / (1.0 + np.exp(-np.concatenate(list(a.astype(np.float64)), axis=1)))
    h = np.zeros(128); H = np.zeros_like(X)
    for c in range(N * W):
        h = G[:, c] * h + X[:, c]; H[:, c] = h
    return {"y": np.stack([H[:, W * r:W * r + W] for r in range(N)]).astype(ml_dtypes.bfloat16)}

@@ -1,0 +1,165 @@
+from concourse.bass import DstId, RemoteDMATransfer
+from concourse.mybir import AluOpType, AxisListType, ActivationFunctionType
+
+N = 7
+W = 32
+SUMMARY = 2
+ON_CHIP_ENGINES = 16
+OFF_CHIP_ENGINES = 8
+
+SCRATCH = {
+    "ax": ("sbuf", [128, 2 * W], "bfloat16"),
+    "hop": ("sbuf", [128, 2 * W], "bfloat16"),
+    "land": ("sbuf", [128, (N - 1) * 2 * W], "bfloat16"),
+    "z": ("sbuf", [128, 2 * N * W], "float32"),
+    "h": ("sbuf", [128, W + 4], "float32"),
+    "yo": ("sbuf", [128, N * W], "bfloat16"),
+}
+SEMAPHORES = ["la", "lx", "loc", "sm", "arrived", "prep", "fin", "st", "sent", "hin"] + [
+    "raw%d" % j for j in range(N - 1)]
+
+
+def _pick(mask, want):
+    bits = [b for b in range(mask.bit_length()) if (mask >> b) & 1]
+    k = 1
+    while 2 * k <= min(want, len(bits)):
+        k *= 2
+    return sum(1 << b for b in bits[:k]), k
+
+
+def _plan(cores, topo):
+    n = len(cores)
+    direct, relay, used = {}, {}, set(cores)
+    for s in range(n):
+        me = cores[s]
+        direct[s] = [d for d in range(s + 1, n) if topo.may_write(me, cores[d])]
+        near = [h for h in range(topo.CHIPS * topo.CORES_PER_CHIP) if topo.chip(h) == topo.chip(me)]
+        near.sort(key=lambda h: (topo.die(h) != topo.die(me), h))
+        for d in range(s + 1, n):
+            if d not in direct[s]:
+                h = [h for h in near if h not in used and topo.may_write(h, cores[d])][0]
+                used.add(h)
+                relay[(s, d)] = h
+    return direct, relay
+
+
+def _layout(d, relay):
+    seg, at, j = {}, 0, 0
+    for s in range(d):
+        if (s, d) in relay:
+            seg[s] = (at, j)
+            at, j = at + W, j + 1
+        else:
+            seg[s] = (at, None)
+            at += SUMMARY
+    return seg, at, at + W
+
+
+def _dst(topo, c):
+    rid, pid, _ = topo.addr(c)
+    return DstId(rid=rid, pnc=pid)
+
+
+def rank_program(g, core, T, topo):
+    cores = list(T.cores)
+    direct, relay = _plan(cores, topo)
+    sem = T.sem
+
+    for (s, d), h in relay.items():
+        if h == core:
+            _, k_in = _pick(topo.mask(cores[s], core), ON_CHIP_ENGINES)
+            m, k = _pick(topo.mask(core, cores[d]), OFF_CHIP_ENGINES)
+            j = _layout(d, relay)[0][s][1]
+            rid, pid, _ = topo.addr(cores[d])
+            g.wait_ge(sem.hin, k_in)
+            g.remote_dma(out_ap=T.land[:, 2 * W * j:2 * W * (j + 1)], in_ap=T.hop[:, :], remote_sem=sem["raw%d" % j],
+                         local_sem=sem.sent, pid=pid, routing_id=rid, dma_engine_mask=m)
+            g.wait_ge(sem.sent, k)
+            return
+
+    r = T.rank_of(core)
+    if r is None:
+        return
+    seg, own, total = _layout(r, relay)
+    helpers = [relay[(r, d)] for d in range(r + 1, len(cores)) if (r, d) in relay]
+    raws = [(at, j, s) for s, (at, j) in seg.items() if j is not None]
+    sigmoid = ActivationFunctionType.Sigmoid
+
+    def xs(at, n):
+        return T.z[:, 2 * at:2 * (at + n):2]
+
+    def gs(at, n):
+        return T.z[:, 2 * at + 1:2 * (at + n):2]
+
+    g.sync.dma_start(T.ax[:, 0:W], T.a[:, :]).then_inc(sem.la, 16)
+    g.scalar.dma_start(T.ax[:, W:2 * W], T.x[:, :]).then_inc(sem.lx, 16)
+
+    sent = 0
+    if helpers:
+        mask = topo.mask(core, helpers[0])
+        for h in helpers:
+            mask &= topo.mask(core, h)
+        m, k = _pick(mask, ON_CHIP_ENGINES)
+        g.wait_ge(sem.la, 16)
+        g.wait_ge(sem.lx, 16)
+        g.remote_dma_fused([RemoteDMATransfer(dst_ids=[_dst(topo, h) for h in helpers], dma_engine_mask=m,
+                                              remote_sem=sem.hin, srcs=[T.ax[:, :]],
+                                              dsts=[T.hop[:, :] for h in helpers])], local_sem=sem.sent)
+        sent += k
+    if direct[r]:
+        mask = topo.mask(core, cores[direct[r][0]])
+        for d in direct[r]:
+            mask &= topo.mask(core, cores[d])
+        m, k = _pick(mask, OFF_CHIP_ENGINES)
+        outs = []
+        for d in direct[r]:
+            at = _layout(d, relay)[0][r][0]
+            outs.append(T.z[:, 2 * at:2 * (at + SUMMARY)])
+        g.wait_ge(sem.sm, 4)
+        g.remote_dma_fused([RemoteDMATransfer(dst_ids=[_dst(topo, cores[d]) for d in direct[r]], dma_engine_mask=m,
+                                              remote_sem=sem.arrived, srcs=[T.h[:, W - 1:W + 3]], dsts=outs)],
+                           local_sem=sem.sent)
+        sent += k
+    if sent:
+        g.wait_ge(sem.sent, sent)
+
+    g.scalar.wait_ge(sem.la, 16)
+    g.scalar.activation(out=gs(own, W), in_=T.ax[:, 0:W], func=sigmoid).then_inc(sem.loc, 1)
+    for at, j, s in raws:
+        _, k = _pick(topo.mask(relay[(s, r)], core), OFF_CHIP_ENGINES)
+        g.scalar.wait_ge(sem["raw%d" % j], k)
+        g.scalar.activation(out=gs(at, W), in_=T.land[:, 2 * W * j:2 * W * j + W], func=sigmoid).then_inc(sem.prep, 1)
+
+    v = g.vector
+    if direct[r]:
+        v.memset(T.h[:, W + 1:W + 2], 0.0).then_inc(sem.sm, 1)
+        v.memset(T.h[:, W + 2:W + 3], 1.0).then_inc(sem.sm, 1)
+    v.wait_ge(sem.lx, 16)
+    v.tensor_copy(out=xs(own, W), in_=T.ax[:, W:2 * W]).then_inc(sem.loc, 1)
+    v.wait_ge(sem.loc, 2)
+    if direct[r]:
+        v.tensor_tensor_scan(out=T.h[:, 0:W], data0=gs(own, W), data1=xs(own, W), initial=0.0,
+                             op0=AluOpType.mult, op1=AluOpType.add).then_inc(sem.sm, 1)
+        v.tensor_reduce(out=T.h[:, W:W + 1], in_=gs(own, W), axis=AxisListType.X,
+                        op=AluOpType.mult).then_inc(sem.sm, 1)
+    for at, j, s in raws:
+        _, k = _pick(topo.mask(relay[(s, r)], core), OFF_CHIP_ENGINES)
+        v.wait_ge(sem["raw%d" % j], k)
+        v.tensor_copy(out=xs(at, W), in_=T.land[:, 2 * W * j + W:2 * W * (j + 1)]).then_inc(sem.prep, 1)
+    if raws:
+        v.wait_ge(sem.prep, 2 * len(raws))
+    summaries = 0
+    for s, (at, j) in seg.items():
+        if j is None:
+            mask = topo.mask(cores[s], core)
+            for d in direct[s]:
+                mask &= topo.mask(cores[s], cores[d])
+            summaries += _pick(mask, OFF_CHIP_ENGINES)[1]
+    if summaries:
+        v.wait_ge(sem.arrived, summaries)
+    v.tensor_tensor_scan(out=T.yo[:, 0:total], data0=gs(0, total), data1=xs(0, total), initial=0.0,
+                         op0=AluOpType.mult, op1=AluOpType.add).then_inc(sem.fin, 1)
+
+    g.sync.wait_ge(sem.fin, 1)
+    g.sync.dma_start(T.y[:, :], T.yo[:, own:total]).then_inc(sem.st, 16)
+    g.sync.wait_ge(sem.st, 16)

@@ -4,22 +4,27 @@ from concourse.mybir import AluOpType, AxisListType, ActivationFunctionType
 N = 7
 W = 32
 SUMMARY = 2
-ON_CHIP_ENGINES = 16
+SUMMARY_DSTS = 2
+ON_CHIP_ENGINES = 8
 OFF_CHIP_ENGINES = 8
 
 SCRATCH = {
     "ax": ("sbuf", [128, 2 * W], "bfloat16"),
-    "hop": ("sbuf", [128, 2 * W], "bfloat16"),
+    "axd": ("dram", [128, 2 * W], "bfloat16"),
+    "hopd": ("dram", [128, 2 * W], "bfloat16"),
     "land": ("sbuf", [128, (N - 1) * 2 * W], "bfloat16"),
     "z": ("sbuf", [128, 2 * N * W], "float32"),
     "h": ("sbuf", [128, W + 4], "float32"),
     "yo": ("sbuf", [128, N * W], "bfloat16"),
 }
-SEMAPHORES = ["la", "lx", "loc", "sm", "arrived", "prep", "fin", "st", "sent", "hin"] + [
+SEMAPHORES = ["la", "lx", "da", "dx", "loc", "sm", "arrived", "prep", "fin", "st", "sent", "hin"] + [
     "raw%d" % j for j in range(N - 1)]
 
 
-def _pick(mask, want):
+def _pick(topo, src, dsts, want):
+    mask = topo.mask(src, dsts[0])
+    for d in dsts:
+        mask &= topo.mask(src, d)
     bits = [b for b in range(mask.bit_length()) if (mask >> b) & 1]
     k = 1
     while 2 * k <= min(want, len(bits)):
@@ -29,29 +34,27 @@ def _pick(mask, want):
 
 def _plan(cores, topo):
     n = len(cores)
-    direct, relay, used = {}, {}, set(cores)
+    short, early, relay, used = {}, {}, {}, set(cores)
     for s in range(n):
         me = cores[s]
-        direct[s] = [d for d in range(s + 1, n) if topo.may_write(me, cores[d])]
+        direct = [d for d in range(s + 1, n) if topo.may_write(me, cores[d])]
+        short[s], early[s] = direct[-SUMMARY_DSTS:], direct[:-SUMMARY_DSTS]
         near = [h for h in range(topo.CHIPS * topo.CORES_PER_CHIP) if topo.chip(h) == topo.chip(me)]
         near.sort(key=lambda h: (topo.die(h) != topo.die(me), h))
         for d in range(s + 1, n):
-            if d not in direct[s]:
+            if d not in direct:
                 h = [h for h in near if h not in used and topo.may_write(h, cores[d])][0]
                 used.add(h)
                 relay[(s, d)] = h
-    return direct, relay
+    return short, early, relay
 
 
-def _layout(d, relay):
-    seg, at, j = {}, 0, 0
+def _layout(d, short):
+    seg, at = {}, 0
     for s in range(d):
-        if (s, d) in relay:
-            seg[s] = (at, j)
-            at, j = at + W, j + 1
-        else:
-            seg[s] = (at, None)
-            at += SUMMARY
+        raw = d not in short[s]
+        seg[s] = (at, raw)
+        at += W if raw else SUMMARY
     return seg, at, at + W
 
 
@@ -62,28 +65,38 @@ def _dst(topo, c):
 
 def rank_program(g, core, T, topo):
     cores = list(T.cores)
-    direct, relay = _plan(cores, topo)
+    short, early, relay = _plan(cores, topo)
     sem = T.sem
+
+    def helpers_of(s):
+        return [relay[(s, d)] for d in range(s + 1, len(cores)) if (s, d) in relay]
+
+    def land(s):
+        return T.land[:, 2 * W * s:2 * W * (s + 1)]
 
     for (s, d), h in relay.items():
         if h == core:
-            _, k_in = _pick(topo.mask(cores[s], core), ON_CHIP_ENGINES)
-            m, k = _pick(topo.mask(core, cores[d]), OFF_CHIP_ENGINES)
-            j = _layout(d, relay)[0][s][1]
+            k_in = _pick(topo, cores[s], helpers_of(s), ON_CHIP_ENGINES)[1]
+            m, k = _pick(topo, core, [cores[d]], OFF_CHIP_ENGINES)
             rid, pid, _ = topo.addr(cores[d])
             g.wait_ge(sem.hin, k_in)
-            g.remote_dma(out_ap=T.land[:, 2 * W * j:2 * W * (j + 1)], in_ap=T.hop[:, :], remote_sem=sem["raw%d" % j],
-                         local_sem=sem.sent, pid=pid, routing_id=rid, dma_engine_mask=m)
+            g.remote_dma(out_ap=land(s), in_ap=T.hopd[:, :], remote_sem=sem["raw%d" % s], local_sem=sem.sent,
+                         pid=pid, routing_id=rid, dma_engine_mask=m)
             g.wait_ge(sem.sent, k)
             return
 
     r = T.rank_of(core)
     if r is None:
         return
-    seg, own, total = _layout(r, relay)
-    helpers = [relay[(r, d)] for d in range(r + 1, len(cores)) if (r, d) in relay]
-    raws = [(at, j, s) for s, (at, j) in seg.items() if j is not None]
+    seg, own, total = _layout(r, short)
+    helpers = helpers_of(r)
     sigmoid = ActivationFunctionType.Sigmoid
+    raws = []
+    for s, (at, raw) in seg.items():
+        if raw and (s, r) in relay:
+            raws.append((at, s, _pick(topo, relay[(s, r)], [core], OFF_CHIP_ENGINES)[1]))
+        elif raw:
+            raws.append((at, s, _pick(topo, cores[s], [cores[d] for d in early[s]], OFF_CHIP_ENGINES)[1]))
 
     def xs(at, n):
         return T.z[:, 2 * at:2 * (at + n):2]
@@ -91,32 +104,36 @@ def rank_program(g, core, T, topo):
     def gs(at, n):
         return T.z[:, 2 * at + 1:2 * (at + n):2]
 
+    if helpers or early[r]:
+        g.sync.dma_start(T.axd[:, 0:W], T.a[:, :]).then_inc(sem.da, 16)
+        g.scalar.dma_start(T.axd[:, W:2 * W], T.x[:, :]).then_inc(sem.dx, 16)
     g.sync.dma_start(T.ax[:, 0:W], T.a[:, :]).then_inc(sem.la, 16)
     g.scalar.dma_start(T.ax[:, W:2 * W], T.x[:, :]).then_inc(sem.lx, 16)
 
     sent = 0
+    if helpers or early[r]:
+        g.wait_ge(sem.da, 16)
+        g.wait_ge(sem.dx, 16)
     if helpers:
-        mask = topo.mask(core, helpers[0])
-        for h in helpers:
-            mask &= topo.mask(core, h)
-        m, k = _pick(mask, ON_CHIP_ENGINES)
-        g.wait_ge(sem.la, 16)
-        g.wait_ge(sem.lx, 16)
+        m, k = _pick(topo, core, helpers, ON_CHIP_ENGINES)
         g.remote_dma_fused([RemoteDMATransfer(dst_ids=[_dst(topo, h) for h in helpers], dma_engine_mask=m,
-                                              remote_sem=sem.hin, srcs=[T.ax[:, :]],
-                                              dsts=[T.hop[:, :] for h in helpers])], local_sem=sem.sent)
+                                              remote_sem=sem.hin, srcs=[T.axd[:, :]],
+                                              dsts=[T.hopd[:, :] for h in helpers])], local_sem=sem.sent)
         sent += k
-    if direct[r]:
-        mask = topo.mask(core, cores[direct[r][0]])
-        for d in direct[r]:
-            mask &= topo.mask(core, cores[d])
-        m, k = _pick(mask, OFF_CHIP_ENGINES)
+    if early[r]:
+        m, k = _pick(topo, core, [cores[d] for d in early[r]], OFF_CHIP_ENGINES)
+        g.remote_dma_fused([RemoteDMATransfer(dst_ids=[_dst(topo, cores[d]) for d in early[r]], dma_engine_mask=m,
+                                              remote_sem=sem["raw%d" % r], srcs=[T.axd[:, :]],
+                                              dsts=[land(r) for d in early[r]])], local_sem=sem.sent)
+        sent += k
+    if short[r]:
+        m, k = _pick(topo, core, [cores[d] for d in short[r]], OFF_CHIP_ENGINES)
         outs = []
-        for d in direct[r]:
-            at = _layout(d, relay)[0][r][0]
+        for d in short[r]:
+            at = _layout(d, short)[0][r][0]
             outs.append(T.z[:, 2 * at:2 * (at + SUMMARY)])
         g.wait_ge(sem.sm, 4)
-        g.remote_dma_fused([RemoteDMATransfer(dst_ids=[_dst(topo, cores[d]) for d in direct[r]], dma_engine_mask=m,
+        g.remote_dma_fused([RemoteDMATransfer(dst_ids=[_dst(topo, cores[d]) for d in short[r]], dma_engine_mask=m,
                                               remote_sem=sem.arrived, srcs=[T.h[:, W - 1:W + 3]], dsts=outs)],
                            local_sem=sem.sent)
         sent += k
@@ -125,36 +142,29 @@ def rank_program(g, core, T, topo):
 
     g.scalar.wait_ge(sem.la, 16)
     g.scalar.activation(out=gs(own, W), in_=T.ax[:, 0:W], func=sigmoid).then_inc(sem.loc, 1)
-    for at, j, s in raws:
-        _, k = _pick(topo.mask(relay[(s, r)], core), OFF_CHIP_ENGINES)
-        g.scalar.wait_ge(sem["raw%d" % j], k)
-        g.scalar.activation(out=gs(at, W), in_=T.land[:, 2 * W * j:2 * W * j + W], func=sigmoid).then_inc(sem.prep, 1)
+    for at, s, k in raws:
+        g.scalar.wait_ge(sem["raw%d" % s], k)
+        g.scalar.activation(out=gs(at, W), in_=T.land[:, 2 * W * s:2 * W * s + W], func=sigmoid).then_inc(sem.prep, 1)
 
     v = g.vector
-    if direct[r]:
+    if short[r]:
         v.memset(T.h[:, W + 1:W + 2], 0.0).then_inc(sem.sm, 1)
         v.memset(T.h[:, W + 2:W + 3], 1.0).then_inc(sem.sm, 1)
     v.wait_ge(sem.lx, 16)
     v.tensor_copy(out=xs(own, W), in_=T.ax[:, W:2 * W]).then_inc(sem.loc, 1)
     v.wait_ge(sem.loc, 2)
-    if direct[r]:
+    if short[r]:
         v.tensor_tensor_scan(out=T.h[:, 0:W], data0=gs(own, W), data1=xs(own, W), initial=0.0,
                              op0=AluOpType.mult, op1=AluOpType.add).then_inc(sem.sm, 1)
         v.tensor_reduce(out=T.h[:, W:W + 1], in_=gs(own, W), axis=AxisListType.X,
                         op=AluOpType.mult).then_inc(sem.sm, 1)
-    for at, j, s in raws:
-        _, k = _pick(topo.mask(relay[(s, r)], core), OFF_CHIP_ENGINES)
-        v.wait_ge(sem["raw%d" % j], k)
-        v.tensor_copy(out=xs(at, W), in_=T.land[:, 2 * W * j + W:2 * W * (j + 1)]).then_inc(sem.prep, 1)
+    for at, s, k in raws:
+        v.wait_ge(sem["raw%d" % s], k)
+        v.tensor_copy(out=xs(at, W), in_=T.land[:, 2 * W * s + W:2 * W * (s + 1)]).then_inc(sem.prep, 1)
     if raws:
         v.wait_ge(sem.prep, 2 * len(raws))
-    summaries = 0
-    for s, (at, j) in seg.items():
-        if j is None:
-            mask = topo.mask(cores[s], core)
-            for d in direct[s]:
-                mask &= topo.mask(cores[s], cores[d])
-            summaries += _pick(mask, OFF_CHIP_ENGINES)[1]
+    summaries = sum(_pick(topo, cores[s], [cores[d] for d in short[s]], OFF_CHIP_ENGINES)[1]
+                    for s, (at, raw) in seg.items() if not raw)
     if summaries:
         v.wait_ge(sem.arrived, summaries)
     v.tensor_tensor_scan(out=T.yo[:, 0:total], data0=gs(0, total), data1=xs(0, total), initial=0.0,

@@ -5,27 +5,32 @@ N = 7
 W = 32
 SUMMARY = 2
 SUMMARY_DSTS = 2
-ON_CHIP_ENGINES = 8
+BLOCK_ENGINES = 2
 OFF_CHIP_ENGINES = 8
+ONE = 30.0
 
 SCRATCH = {
     "ax": ("sbuf", [128, 2 * W], "bfloat16"),
-    "axd": ("dram", [128, 2 * W], "bfloat16"),
-    "hopd": ("dram", [128, 2 * W], "bfloat16"),
+    "srcd": ("dram", [2, 128, W], "bfloat16"),
+    "hopd": ("dram", [128, W], "bfloat16"),
+    "hs": ("sbuf", [128, 2 * SUMMARY], "float32"),
     "land": ("sbuf", [128, (N - 1) * 2 * W], "bfloat16"),
+    "la": ("sbuf", [128, (N - 1) * W], "bfloat16"),
+    "lx": ("sbuf", [128, (N - 1) * W], "bfloat16"),
     "z": ("sbuf", [128, 2 * N * W], "float32"),
     "h": ("sbuf", [128, W + 4], "float32"),
     "yo": ("sbuf", [128, N * W], "bfloat16"),
 }
-SEMAPHORES = ["la", "lx", "da", "dx", "loc", "sm", "arrived", "prep", "fin", "st", "sent", "hin"] + [
-    "raw%d" % j for j in range(N - 1)]
+SEMAPHORES = ["la", "lx", "da", "dx", "loc", "z0", "sm", "arrived", "prep", "fin", "st", "sent", "hin", "hsum"] + [
+    "%s%d" % (n, j) for n in ("raw", "ra", "rx") for j in range(N - 1)]
 
 
-def _pick(topo, src, dsts, want):
+def _pick(topo, src, dsts, want, skip=0, avoid=0):
     mask = topo.mask(src, dsts[0])
     for d in dsts:
         mask &= topo.mask(src, d)
     bits = [b for b in range(mask.bit_length()) if (mask >> b) & 1]
+    bits = ([b for b in bits if not (avoid >> b) & 1] + [b for b in bits if (avoid >> b) & 1])[skip:]
     k = 1
     while 2 * k <= min(want, len(bits)):
         k *= 2
@@ -34,25 +39,25 @@ def _pick(topo, src, dsts, want):
 
 def _plan(cores, topo):
     n = len(cores)
-    short, early, relay, used = {}, {}, {}, set(cores)
+    short, early, near, far, role = {}, {}, {}, {}, {}
     for s in range(n):
         me = cores[s]
         direct = [d for d in range(s + 1, n) if topo.may_write(me, cores[d])]
+        cross = [d for d in range(s + 1, n) if d not in direct]
         short[s], early[s] = direct[-SUMMARY_DSTS:], direct[:-SUMMARY_DSTS]
-        near = [h for h in range(topo.CHIPS * topo.CORES_PER_CHIP) if topo.chip(h) == topo.chip(me)]
-        near.sort(key=lambda h: (topo.die(h) != topo.die(me), h))
-        for d in range(s + 1, n):
-            if d not in direct:
-                h = [h for h in near if h not in used and topo.may_write(h, cores[d])][0]
-                used.add(h)
-                relay[(s, d)] = h
-    return short, early, relay
+        near[s], far[s] = (cross[0] if cross else None), cross[1:]
+        ports = [h for h in range(topo.CHIPS * topo.CORES_PER_CHIP)
+                 if topo.chip(h) == topo.chip(me) and h not in cores and all(topo.may_write(h, cores[d]) for d in cross)]
+        ports.sort(key=lambda h: (topo.die(h) != topo.die(me), h))
+        if cross:
+            role[ports[0]], role[ports[1]] = ("a", s), ("x", s)
+    return short, early, near, far, role
 
 
-def _layout(d, short):
+def _layout(d, early, near):
     seg, at = {}, 0
     for s in range(d):
-        raw = d not in short[s]
+        raw = d in early[s] or d == near[s]
         seg[s] = (at, raw)
         at += W if raw else SUMMARY
     return seg, at, at + W
@@ -65,38 +70,78 @@ def _dst(topo, c):
 
 def rank_program(g, core, T, topo):
     cores = list(T.cores)
-    short, early, relay = _plan(cores, topo)
+    short, early, near, far, role = _plan(cores, topo)
     sem = T.sem
+    helper = {(kind, s): h for h, (kind, s) in role.items()}
 
-    def helpers_of(s):
-        return [relay[(s, d)] for d in range(s + 1, len(cores)) if (s, d) in relay]
+    def slot(d, s):
+        at = _layout(d, early, near)[0][s][0]
+        return T.z[:, 2 * at:2 * (at + SUMMARY)]
 
-    def land(s):
-        return T.land[:, 2 * W * s:2 * W * (s + 1)]
+    def off(s):
+        return topo.mask(cores[s], [c for c in cores if topo.chip(c) != topo.chip(cores[s])][0])
 
-    for (s, d), h in relay.items():
-        if h == core:
-            k_in = _pick(topo, cores[s], helpers_of(s), ON_CHIP_ENGINES)[1]
-            m, k = _pick(topo, core, [cores[d]], OFF_CHIP_ENGINES)
-            rid, pid, _ = topo.addr(cores[d])
-            g.wait_ge(sem.hin, k_in)
-            g.remote_dma(out_ap=land(s), in_ap=T.hopd[:, :], remote_sem=sem["raw%d" % s], local_sem=sem.sent,
-                         pid=pid, routing_id=rid, dma_engine_mask=m)
-            g.wait_ge(sem.sent, k)
-            return
+    def k_block(s, kind):
+        return _pick(topo, cores[s], [helper[(kind, s)]], BLOCK_ENGINES, 0 if kind == "a" else BLOCK_ENGINES, off(s))
+
+    def carried(s, kind):
+        return far[s][0::2] if kind == "x" else far[s][1::2]
+
+    def carriers(s):
+        return [helper[(kind, s)] for kind in ("x", "a") if carried(s, kind)]
+
+    def k_sum(s):
+        return _pick(topo, cores[s], carriers(s), 2 * BLOCK_ENGINES, 0, off(s))
+
+    if core in role:
+        kind, s = role[core]
+        to = cores[near[s]]
+        m, k = _pick(topo, core, [to], OFF_CHIP_ENGINES)
+        rid, pid, _ = topo.addr(to)
+        g.wait_ge(sem.hin, k_block(s, kind)[1])
+        g.remote_dma(out_ap=T["l" + kind][:, W * s:W * (s + 1)], in_ap=T.hopd[:, :],
+                     remote_sem=sem["r%s%d" % (kind, s)], local_sem=sem.sent, pid=pid, routing_id=rid,
+                     dma_engine_mask=m)
+        sent = k
+        if carried(s, kind):
+            to = [cores[d] for d in carried(s, kind)]
+            m, k = _pick(topo, core, to, OFF_CHIP_ENGINES)
+            g.wait_ge(sem.hsum, k_sum(s)[1])
+            g.remote_dma_fused([RemoteDMATransfer(dst_ids=[_dst(topo, c) for c in to], dma_engine_mask=m,
+                                                  remote_sem=sem.arrived, srcs=[T.hs[:, :]],
+                                                  dsts=[slot(d, s) for d in carried(s, kind)])], local_sem=sem.sent)
+            sent += k
+        g.wait_ge(sem.sent, sent)
+        return
 
     r = T.rank_of(core)
     if r is None:
         return
-    seg, own, total = _layout(r, short)
-    helpers = helpers_of(r)
+    seg, own, total = _layout(r, early, near)
     sigmoid = ActivationFunctionType.Sigmoid
-    raws = []
+    summing = bool(short[r] or far[r])
+
+    raws, last = [], None
     for s, (at, raw) in seg.items():
-        if raw and (s, r) in relay:
-            raws.append((at, s, _pick(topo, relay[(s, r)], [core], OFF_CHIP_ENGINES)[1]))
-        elif raw:
-            raws.append((at, s, _pick(topo, cores[s], [cores[d] for d in early[s]], OFF_CHIP_ENGINES)[1]))
+        if not raw:
+            continue
+        if r in early[s]:
+            k = _pick(topo, cores[s], [cores[d] for d in early[s]], OFF_CHIP_ENGINES)[1]
+            raws.append([at, W, T.land[:, 2 * W * s:2 * W * s + W], T.land[:, 2 * W * s + W:2 * W * (s + 1)],
+                         [("raw%d" % s, k)], [("raw%d" % s, k)]])
+            continue
+        ka = _pick(topo, helper[("a", s)], [core], OFF_CHIP_ENGINES)[1]
+        kx = _pick(topo, helper[("x", s)], [core], OFF_CHIP_ENGINES)[1]
+        if last is not None and last[1] == s and last[0][0] + last[0][1] == at:
+            e, s0 = last[0], last[2]
+            e[1] += W
+            e[4].append(("ra%d" % s, ka))
+            e[5].append(("rx%d" % s, kx))
+        else:
+            e, s0 = [at, W, None, None, [("ra%d" % s, ka)], [("rx%d" % s, kx)]], s
+            raws.append(e)
+        e[2], e[3] = T.la[:, W * s0:W * (s + 1)], T.lx[:, W * s0:W * (s + 1)]
+        last = (e, s + 1, s0)
 
     def xs(at, n):
         return T.z[:, 2 * at:2 * (at + n):2]
@@ -104,67 +149,86 @@ def rank_program(g, core, T, topo):
     def gs(at, n):
         return T.z[:, 2 * at + 1:2 * (at + n):2]
 
-    if helpers or early[r]:
-        g.sync.dma_start(T.axd[:, 0:W], T.a[:, :]).then_inc(sem.da, 16)
-        g.scalar.dma_start(T.axd[:, W:2 * W], T.x[:, :]).then_inc(sem.dx, 16)
+    if near[r] is not None:
+        g.sync.dma_start(T.srcd[0], T.a[:, :]).then_inc(sem.da, 16)
+        g.scalar.dma_start(T.srcd[1], T.x[:, :]).then_inc(sem.dx, 16)
     g.sync.dma_start(T.ax[:, 0:W], T.a[:, :]).then_inc(sem.la, 16)
     g.scalar.dma_start(T.ax[:, W:2 * W], T.x[:, :]).then_inc(sem.lx, 16)
 
     sent = 0
-    if helpers or early[r]:
+    if near[r] is not None:
         g.wait_ge(sem.da, 16)
         g.wait_ge(sem.dx, 16)
-    if helpers:
-        m, k = _pick(topo, core, helpers, ON_CHIP_ENGINES)
-        g.remote_dma_fused([RemoteDMATransfer(dst_ids=[_dst(topo, h) for h in helpers], dma_engine_mask=m,
-                                              remote_sem=sem.hin, srcs=[T.axd[:, :]],
-                                              dsts=[T.hopd[:, :] for h in helpers])], local_sem=sem.sent)
-        sent += k
+        hop = []
+        for i, kind in enumerate(("a", "x")):
+            m, k = k_block(r, kind)
+            hop.append(RemoteDMATransfer(dst_ids=[_dst(topo, helper[(kind, r)])], dma_engine_mask=m,
+                                         remote_sem=sem.hin, srcs=[T.srcd[i]], dsts=[T.hopd[:, :]]))
+            sent += k
+        g.remote_dma_fused(hop, local_sem=sem.sent)
     if early[r]:
         m, k = _pick(topo, core, [cores[d] for d in early[r]], OFF_CHIP_ENGINES)
+        g.wait_ge(sem.la, 16)
+        g.wait_ge(sem.lx, 16)
         g.remote_dma_fused([RemoteDMATransfer(dst_ids=[_dst(topo, cores[d]) for d in early[r]], dma_engine_mask=m,
-                                              remote_sem=sem["raw%d" % r], srcs=[T.axd[:, :]],
-                                              dsts=[land(r) for d in early[r]])], local_sem=sem.sent)
+                                              remote_sem=sem["raw%d" % r], srcs=[T.ax[:, :]],
+                                              dsts=[T.land[:, 2 * W * r:2 * W * (r + 1)] for d in early[r]])],
+                           local_sem=sem.sent)
+        sent += k
+    if far[r]:
+        m, k = k_sum(r)
+        g.wait_ge(sem.z0, 1)
+        g.wait_ge(sem.sm, 3)
+        g.remote_dma_fused([RemoteDMATransfer(dst_ids=[_dst(topo, h) for h in carriers(r)], dma_engine_mask=m,
+                                              remote_sem=sem.hsum, srcs=[T.h[:, W - 1:W + 3]],
+                                              dsts=[T.hs[:, :] for h in carriers(r)])], local_sem=sem.sent)
         sent += k
     if short[r]:
         m, k = _pick(topo, core, [cores[d] for d in short[r]], OFF_CHIP_ENGINES)
-        outs = []
-        for d in short[r]:
-            at = _layout(d, short)[0][r][0]
-            outs.append(T.z[:, 2 * at:2 * (at + SUMMARY)])
-        g.wait_ge(sem.sm, 4)
+        g.wait_ge(sem.z0, 1)
+        g.wait_ge(sem.sm, 3)
         g.remote_dma_fused([RemoteDMATransfer(dst_ids=[_dst(topo, cores[d]) for d in short[r]], dma_engine_mask=m,
-                                              remote_sem=sem.arrived, srcs=[T.h[:, W - 1:W + 3]], dsts=outs)],
-                           local_sem=sem.sent)
+                                              remote_sem=sem.arrived, srcs=[T.h[:, W - 1:W + 3]],
+                                              dsts=[slot(d, r) for d in short[r]])], local_sem=sem.sent)
         sent += k
     if sent:
         g.wait_ge(sem.sent, sent)
 
+    if summing:
+        g.scalar.wait_ge(sem.z0, 1)
+        g.scalar.activation(out=T.h[:, W + 2:W + 3], in_=T.h[:, W + 1:W + 2], func=sigmoid,
+                            bias=ONE).then_inc(sem.sm, 1)
     g.scalar.wait_ge(sem.la, 16)
     g.scalar.activation(out=gs(own, W), in_=T.ax[:, 0:W], func=sigmoid).then_inc(sem.loc, 1)
-    for at, s, k in raws:
-        g.scalar.wait_ge(sem["raw%d" % s], k)
-        g.scalar.activation(out=gs(at, W), in_=T.land[:, 2 * W * s:2 * W * s + W], func=sigmoid).then_inc(sem.prep, 1)
+    for at, n, a_in, x_in, wa, wx in raws:
+        for name, k in wa:
+            g.scalar.wait_ge(sem[name], k)
+        g.scalar.activation(out=gs(at, n), in_=a_in, func=sigmoid).then_inc(sem.prep, 1)
 
     v = g.vector
-    if short[r]:
-        v.memset(T.h[:, W + 1:W + 2], 0.0).then_inc(sem.sm, 1)
-        v.memset(T.h[:, W + 2:W + 3], 1.0).then_inc(sem.sm, 1)
+    if summing:
+        v.memset(T.h[:, W + 1:W + 2], 0.0).then_inc(sem.z0, 1)
     v.wait_ge(sem.lx, 16)
     v.tensor_copy(out=xs(own, W), in_=T.ax[:, W:2 * W]).then_inc(sem.loc, 1)
     v.wait_ge(sem.loc, 2)
-    if short[r]:
+    if summing:
         v.tensor_tensor_scan(out=T.h[:, 0:W], data0=gs(own, W), data1=xs(own, W), initial=0.0,
                              op0=AluOpType.mult, op1=AluOpType.add).then_inc(sem.sm, 1)
         v.tensor_reduce(out=T.h[:, W:W + 1], in_=gs(own, W), axis=AxisListType.X,
                         op=AluOpType.mult).then_inc(sem.sm, 1)
-    for at, s, k in raws:
-        v.wait_ge(sem["raw%d" % s], k)
-        v.tensor_copy(out=xs(at, W), in_=T.land[:, 2 * W * s + W:2 * W * (s + 1)]).then_inc(sem.prep, 1)
+    for at, n, a_in, x_in, wa, wx in raws:
+        for name, k in wx:
+            v.wait_ge(sem[name], k)
+        v.tensor_copy(out=xs(at, n), in_=x_in).then_inc(sem.prep, 1)
     if raws:
         v.wait_ge(sem.prep, 2 * len(raws))
-    summaries = sum(_pick(topo, cores[s], [cores[d] for d in short[s]], OFF_CHIP_ENGINES)[1]
-                    for s, (at, raw) in seg.items() if not raw)
+    summaries = 0
+    for s, (at, raw) in seg.items():
+        if not raw and r in short[s]:
+            summaries += _pick(topo, cores[s], [cores[d] for d in short[s]], OFF_CHIP_ENGINES)[1]
+        elif not raw:
+            kind = "x" if r in carried(s, "x") else "a"
+            summaries += _pick(topo, helper[(kind, s)], [cores[d] for d in carried(s, kind)], OFF_CHIP_ENGINES)[1]
     if summaries:
         v.wait_ge(sem.arrived, summaries)
     v.tensor_tensor_scan(out=T.yo[:, 0:total], data0=gs(0, total), data1=xs(0, total), initial=0.0,

from concourse.bass import DstId, RemoteDMATransfer
from concourse.mybir import AluOpType, AxisListType, ActivationFunctionType

N = 7
W = 32
SUMMARY = 2
SUMMARY_DSTS = 2
BLOCK_ENGINES = 2
OFF_CHIP_ENGINES = 8
ONE = 30.0

SCRATCH = {
    "ax": ("sbuf", [128, 2 * W], "bfloat16"),
    "srcd": ("dram", [2, 128, W], "bfloat16"),
    "hopd": ("dram", [128, W], "bfloat16"),
    "hs": ("sbuf", [128, 2 * SUMMARY], "float32"),
    "land": ("sbuf", [128, (N - 1) * 2 * W], "bfloat16"),
    "la": ("sbuf", [128, (N - 1) * W], "bfloat16"),
    "lx": ("sbuf", [128, (N - 1) * W], "bfloat16"),
    "z": ("sbuf", [128, 2 * N * W], "float32"),
    "h": ("sbuf", [128, W + 4], "float32"),
    "yo": ("sbuf", [128, N * W], "bfloat16"),
}
SEMAPHORES = ["la", "lx", "da", "dx", "loc", "z0", "sm", "arrived", "prep", "fin", "st", "sent", "hin", "hsum"] + [
    "%s%d" % (n, j) for n in ("raw", "ra", "rx") for j in range(N - 1)]


def _pick(topo, src, dsts, want, skip=0, avoid=0):
    mask = topo.mask(src, dsts[0])
    for d in dsts:
        mask &= topo.mask(src, d)
    bits = [b for b in range(mask.bit_length()) if (mask >> b) & 1]
    bits = ([b for b in bits if not (avoid >> b) & 1] + [b for b in bits if (avoid >> b) & 1])[skip:]
    k = 1
    while 2 * k <= min(want, len(bits)):
        k *= 2
    return sum(1 << b for b in bits[:k]), k


def _plan(cores, topo):
    n = len(cores)
    short, early, near, far, role = {}, {}, {}, {}, {}
    for s in range(n):
        me = cores[s]
        direct = [d for d in range(s + 1, n) if topo.may_write(me, cores[d])]
        cross = [d for d in range(s + 1, n) if d not in direct]
        short[s], early[s] = direct[-SUMMARY_DSTS:], direct[:-SUMMARY_DSTS]
        near[s], far[s] = (cross[0] if cross else None), cross[1:]
        ports = [h for h in range(topo.CHIPS * topo.CORES_PER_CHIP)
                 if topo.chip(h) == topo.chip(me) and h not in cores and all(topo.may_write(h, cores[d]) for d in cross)]
        ports.sort(key=lambda h: (topo.die(h) != topo.die(me), h))
        if cross:
            role[ports[0]], role[ports[1]] = ("a", s), ("x", s)
    return short, early, near, far, role


def _layout(d, early, near):
    seg, at = {}, 0
    for s in range(d):
        raw = d in early[s] or d == near[s]
        seg[s] = (at, raw)
        at += W if raw else SUMMARY
    return seg, at, at + W


def _dst(topo, c):
    rid, pid, _ = topo.addr(c)
    return DstId(rid=rid, pnc=pid)


def rank_program(g, core, T, topo):
    cores = list(T.cores)
    short, early, near, far, role = _plan(cores, topo)
    sem = T.sem
    helper = {(kind, s): h for h, (kind, s) in role.items()}

    def slot(d, s):
        at = _layout(d, early, near)[0][s][0]
        return T.z[:, 2 * at:2 * (at + SUMMARY)]

    def off(s):
        return topo.mask(cores[s], [c for c in cores if topo.chip(c) != topo.chip(cores[s])][0])

    def k_block(s, kind):
        return _pick(topo, cores[s], [helper[(kind, s)]], BLOCK_ENGINES, 0 if kind == "a" else BLOCK_ENGINES, off(s))

    def carried(s, kind):
        return far[s][0::2] if kind == "x" else far[s][1::2]

    def carriers(s):
        return [helper[(kind, s)] for kind in ("x", "a") if carried(s, kind)]

    def k_sum(s):
        return _pick(topo, cores[s], carriers(s), 2 * BLOCK_ENGINES, 0, off(s))

    if core in role:
        kind, s = role[core]
        to = cores[near[s]]
        m, k = _pick(topo, core, [to], OFF_CHIP_ENGINES)
        rid, pid, _ = topo.addr(to)
        g.wait_ge(sem.hin, k_block(s, kind)[1])
        g.remote_dma(out_ap=T["l" + kind][:, W * s:W * (s + 1)], in_ap=T.hopd[:, :],
                     remote_sem=sem["r%s%d" % (kind, s)], local_sem=sem.sent, pid=pid, routing_id=rid,
                     dma_engine_mask=m)
        sent = k
        if carried(s, kind):
            to = [cores[d] for d in carried(s, kind)]
            m, k = _pick(topo, core, to, OFF_CHIP_ENGINES)
            g.wait_ge(sem.hsum, k_sum(s)[1])
            g.remote_dma_fused([RemoteDMATransfer(dst_ids=[_dst(topo, c) for c in to], dma_engine_mask=m,
                                                  remote_sem=sem.arrived, srcs=[T.hs[:, :]],
                                                  dsts=[slot(d, s) for d in carried(s, kind)])], local_sem=sem.sent)
            sent += k
        g.wait_ge(sem.sent, sent)
        return

    r = T.rank_of(core)
    if r is None:
        return
    seg, own, total = _layout(r, early, near)
    sigmoid = ActivationFunctionType.Sigmoid
    summing = bool(short[r] or far[r])

    raws, last = [], None
    for s, (at, raw) in seg.items():
        if not raw:
            continue
        if r in early[s]:
            k = _pick(topo, cores[s], [cores[d] for d in early[s]], OFF_CHIP_ENGINES)[1]
            raws.append([at, W, T.land[:, 2 * W * s:2 * W * s + W], T.land[:, 2 * W * s + W:2 * W * (s + 1)],
                         [("raw%d" % s, k)], [("raw%d" % s, k)]])
            continue
        ka = _pick(topo, helper[("a", s)], [core], OFF_CHIP_ENGINES)[1]
        kx = _pick(topo, helper[("x", s)], [core], OFF_CHIP_ENGINES)[1]
        if last is not None and last[1] == s and last[0][0] + last[0][1] == at:
            e, s0 = last[0], last[2]
            e[1] += W
            e[4].append(("ra%d" % s, ka))
            e[5].append(("rx%d" % s, kx))
        else:
            e, s0 = [at, W, None, None, [("ra%d" % s, ka)], [("rx%d" % s, kx)]], s
            raws.append(e)
        e[2], e[3] = T.la[:, W * s0:W * (s + 1)], T.lx[:, W * s0:W * (s + 1)]
        last = (e, s + 1, s0)

    def xs(at, n):
        return T.z[:, 2 * at:2 * (at + n):2]

    def gs(at, n):
        return T.z[:, 2 * at + 1:2 * (at + n):2]

    if near[r] is not None:
        g.sync.dma_start(T.srcd[0], T.a[:, :]).then_inc(sem.da, 16)
        g.scalar.dma_start(T.srcd[1], T.x[:, :]).then_inc(sem.dx, 16)
    g.sync.dma_start(T.ax[:, 0:W], T.a[:, :]).then_inc(sem.la, 16)
    g.scalar.dma_start(T.ax[:, W:2 * W], T.x[:, :]).then_inc(sem.lx, 16)

    sent = 0
    if near[r] is not None:
        g.wait_ge(sem.da, 16)
        g.wait_ge(sem.dx, 16)
        hop = []
        for i, kind in enumerate(("a", "x")):
            m, k = k_block(r, kind)
            hop.append(RemoteDMATransfer(dst_ids=[_dst(topo, helper[(kind, r)])], dma_engine_mask=m,
                                         remote_sem=sem.hin, srcs=[T.srcd[i]], dsts=[T.hopd[:, :]]))
            sent += k
        g.remote_dma_fused(hop, local_sem=sem.sent)
    if early[r]:
        m, k = _pick(topo, core, [cores[d] for d in early[r]], OFF_CHIP_ENGINES)
        g.wait_ge(sem.la, 16)
        g.wait_ge(sem.lx, 16)
        g.remote_dma_fused([RemoteDMATransfer(dst_ids=[_dst(topo, cores[d]) for d in early[r]], dma_engine_mask=m,
                                              remote_sem=sem["raw%d" % r], srcs=[T.ax[:, :]],
                                              dsts=[T.land[:, 2 * W * r:2 * W * (r + 1)] for d in early[r]])],
                           local_sem=sem.sent)
        sent += k
    if far[r]:
        m, k = k_sum(r)
        g.wait_ge(sem.z0, 1)
        g.wait_ge(sem.sm, 3)
        g.remote_dma_fused([RemoteDMATransfer(dst_ids=[_dst(topo, h) for h in carriers(r)], dma_engine_mask=m,
                                              remote_sem=sem.hsum, srcs=[T.h[:, W - 1:W + 3]],
                                              dsts=[T.hs[:, :] for h in carriers(r)])], local_sem=sem.sent)
        sent += k
    if short[r]:
        m, k = _pick(topo, core, [cores[d] for d in short[r]], OFF_CHIP_ENGINES)
        g.wait_ge(sem.z0, 1)
        g.wait_ge(sem.sm, 3)
        g.remote_dma_fused([RemoteDMATransfer(dst_ids=[_dst(topo, cores[d]) for d in short[r]], dma_engine_mask=m,
                                              remote_sem=sem.arrived, srcs=[T.h[:, W - 1:W + 3]],
                                              dsts=[slot(d, r) for d in short[r]])], local_sem=sem.sent)
        sent += k
    if sent:
        g.wait_ge(sem.sent, sent)

    if summing:
        g.scalar.wait_ge(sem.z0, 1)
        g.scalar.activation(out=T.h[:, W + 2:W + 3], in_=T.h[:, W + 1:W + 2], func=sigmoid,
                            bias=ONE).then_inc(sem.sm, 1)
    g.scalar.wait_ge(sem.la, 16)
    g.scalar.activation(out=gs(own, W), in_=T.ax[:, 0:W], func=sigmoid).then_inc(sem.loc, 1)
    for at, n, a_in, x_in, wa, wx in raws:
        for name, k in wa:
            g.scalar.wait_ge(sem[name], k)
        g.scalar.activation(out=gs(at, n), in_=a_in, func=sigmoid).then_inc(sem.prep, 1)

    v = g.vector
    if summing:
        v.memset(T.h[:, W + 1:W + 2], 0.0).then_inc(sem.z0, 1)
    v.wait_ge(sem.lx, 16)
    v.tensor_copy(out=xs(own, W), in_=T.ax[:, W:2 * W]).then_inc(sem.loc, 1)
    v.wait_ge(sem.loc, 2)
    if summing:
        v.tensor_tensor_scan(out=T.h[:, 0:W], data0=gs(own, W), data1=xs(own, W), initial=0.0,
                             op0=AluOpType.mult, op1=AluOpType.add).then_inc(sem.sm, 1)
        v.tensor_reduce(out=T.h[:, W:W + 1], in_=gs(own, W), axis=AxisListType.X,
                        op=AluOpType.mult).then_inc(sem.sm, 1)
    for at, n, a_in, x_in, wa, wx in raws:
        for name, k in wx:
            v.wait_ge(sem[name], k)
        v.tensor_copy(out=xs(at, n), in_=x_in).then_inc(sem.prep, 1)
    if raws:
        v.wait_ge(sem.prep, 2 * len(raws))
    summaries = 0
    for s, (at, raw) in seg.items():
        if not raw and r in short[s]:
            summaries += _pick(topo, cores[s], [cores[d] for d in short[s]], OFF_CHIP_ENGINES)[1]
        elif not raw:
            kind = "x" if r in carried(s, "x") else "a"
            summaries += _pick(topo, helper[(kind, s)], [cores[d] for d in carried(s, kind)], OFF_CHIP_ENGINES)[1]
    if summaries:
        v.wait_ge(sem.arrived, summaries)
    v.tensor_tensor_scan(out=T.yo[:, 0:total], data0=gs(0, total), data1=xs(0, total), initial=0.0,
                         op0=AluOpType.mult, op1=AluOpType.add).then_inc(sem.fin, 1)

    g.sync.wait_ge(sem.fin, 1)
    g.sync.dma_start(T.y[:, :], T.yo[:, own:total]).then_inc(sem.st, 16)
    g.sync.wait_ge(sem.st, 16)
